import numpy as np
import ml_dtypes


def mxq(x, axis, fmt="e4m3"):
    dtype, down = {"e4m3": (ml_dtypes.float8_e4m3fn, 7), "e5m2": (ml_dtypes.float8_e5m2, 14)}[fmt]
    v = np.moveaxis(np.asarray(x, np.float32).astype(ml_dtypes.bfloat16).astype(np.float64), axis, -1)
    blocks = v.reshape(v.shape[:-1] + (-1, 32))
    amax = np.abs(blocks).max(-1, keepdims=True)
    byte = np.maximum(np.where(amax > 0, np.frexp(amax)[1] - 1 + 127, 0) - down, 1)
    scale = np.exp2(byte - 127.0)
    codes = (blocks / scale).astype(np.float32).astype(dtype).astype(np.float64)
    return np.moveaxis((codes * scale).reshape(v.shape), -1, axis)


WIDE = False


def mx_kscale(k):
    if not WIDE:
        return np.ones(k)
    levels = np.array([10, -10, 5, -5, 0])
    if k % 512:
        return np.exp2(np.random.permutation(np.resize(levels, k // 32))).repeat(32)
    a = np.empty((k // 512, 16))
    for p in range(k // 512):
        a[p, :8] = np.random.permutation(np.resize(levels, 8))
        for g in range(8):
            far = levels[np.abs(levels - a[p, g]) >= 10]
            a[p, g + 8] = far[np.random.randint(len(far))]
    return np.exp2(a.ravel()).repeat(32)


def f64(x):
    return np.asarray(x).astype(np.float64)


def striped(idx):
    return np.tile(idx.reshape(-1, 16).T, (8, 1)).astype(np.uint16)


def unstriped(offs):
    return offs[:16].T.reshape(-1).astype(np.int64)


def striped8(idx):
    return np.concatenate([x.reshape(-1, 16).T for x in idx]).astype(np.uint16)


def runs(offs, k):
    lists = np.stack([offs[16 * r : 16 * r + 16].T.reshape(-1) for r in range(8)]).astype(np.int64)
    return lists[np.arange(k) % 512 // 64]


def pack_weight(w):
    k, n = w.shape
    w = f64(np.asarray(w, np.float32).astype(ml_dtypes.bfloat16)).reshape(k // 32, 32, n)
    amax = np.abs(w).max(1)
    byte = np.clip(np.where(amax > 0, np.frexp(amax)[1] - 1 + 127 - 7, 1), 1, 254)
    scaled = (w * np.exp2(127.0 - byte)[:, None, :]).reshape(k, n).astype(np.float32)
    words = np.ascontiguousarray(scaled.reshape(k // 512, 128, 4, n).transpose(0, 1, 3, 2)).astype(ml_dtypes.float8_e4m3fn).view(np.uint8)
    return words, np.ascontiguousarray(byte.astype(np.uint8).reshape(k // 512, 16, n))


def unpack_weight(words, scales):
    g, p, n, _ = words.shape
    vals = np.ascontiguousarray(words).view(ml_dtypes.float8_e4m3fn).astype(np.float64) * np.repeat(np.exp2(scales.astype(np.float64) - 127.0), 8, axis=1)[..., None]
    return vals.transpose(0, 1, 3, 2).reshape(g * 512, n)

def planes(y):
    n, m = y.shape
    v = y.astype(np.float32).astype(ml_dtypes.bfloat16).astype(np.float64).reshape(n // 32, 32, m)
    top = np.abs(v).max(1)
    byte = np.clip(np.where(top > 0, np.frexp(top)[1] - 1 + 127 - 7, 1), 1, 254)
    codes = (v * np.exp2(127.0 - byte)[:, None, :]).reshape(n, m).astype(np.float32).astype(ml_dtypes.float8_e4m3fn).view(np.uint8)
    words = codes.reshape(n // 512, 128, 4, m).transpose(0, 1, 3, 2)
    return np.ascontiguousarray(words), np.ascontiguousarray(byte.astype(np.uint8).reshape(n // 512, 16, m))


K, T, S, H, G = 512, 2048, 512, 512, 2048


def setup_inputs():
    n = np.random.standard_normal
    s = mx_kscale(K)[:, None]
    packed_xT = pack_weight(n((K, T)) * s)
    packed_w1 = pack_weight(n((K, H)) / np.sqrt(K) / s)
    packed_dT = pack_weight(n((K, G)) / s)
    return {
        "x_words": packed_xT[0],
        "x_scales": packed_xT[1],
        "w1_words": packed_w1[0],
        "w1_scales": packed_w1[1],
        "gs": (np.random.uniform(0.5, 1.5, (K, 1)) * s).astype(np.float32),
        "d_words": packed_dT[0],
        "d_scales": packed_dT[1],
        "offs": striped(np.random.permutation(T)[:S]),
        "rt": striped8(np.stack([np.random.permutation(S) for _ in range(8)])),
        "lf": striped8(np.stack([np.random.permutation(S) for _ in range(8)])),
        "kq": striped8(np.random.randint(0, G, (8, H))),
    }


def reference(x_words, x_scales, w1_words, w1_scales, gs, d_words, d_scales, offs, rt, lf, kq):
    d_kq = unpack_weight(d_words, d_scales)[np.arange(K)[:, None], runs(kq, K)]
    xq = unpack_weight(x_words, x_scales)[:, unstriped(offs)]
    y = unpack_weight(w1_words, w1_scales).T @ xq
    a = y[np.arange(H)[:, None], runs(rt, H)]
    uh = 0.5 * (y + a) - (0.25 * ((a) ** 2) - (0.25 * ((y) ** 2)))
    un = uh[np.arange(H)[:, None], runs(lf, H)]
    z = f64(gs) * (0.25 * ((uh) ** 2) - (0.25 * ((un) ** 2)))
    out_0 = 0.0625 * ((d_kq.T @ mxq(z, 0, "e4m3")))
    return (out_0,) + planes(out_0)

@@ -1,0 +1,225 @@
+from contextlib import ExitStack
+
+import concourse.mybir as mybir
+
+K, T, S, H, G = 512, 2048, 512, 512, 2048
+FLOPS = 2 * K * H * S * 2
+
+F32 = mybir.dt.float32
+BF16 = mybir.dt.bfloat16
+I32 = mybir.dt.int32
+U32 = mybir.dt.uint32
+U16 = mybir.dt.uint16
+U8 = mybir.dt.uint8
+FP8X4 = mybir.dt.float8_e4m3fn_x4
+ALU = mybir.AluOpType
+ACT = mybir.ActivationFunctionType
+
+P = 128
+PACK = 4
+HALF = S // 2
+PIECE = 128
+PIECES = S // PIECE
+
+
+def tile_picked_wendroff_none_po_kernel(
+    tc, x_words, x_scales, w1_words, w1_scales, gs, d_words, d_scales, offs, rt, lf, kq, out_0, out_1, out_2
+):
+    nc = tc.nc
+
+    def as_words(dram):
+        return dram[0].rearrange("p n t -> p (n t)").bitcast(I32)
+
+    def dealt(ap):
+        return ap.rearrange("p (m t) -> p t m", t=PACK)
+
+    def planes(ap):
+        return ap.rearrange("p (t m) -> p t m", t=PACK)
+
+    def entries(offsets, first, count):
+        return offsets[:, first // 16 : (first + count) // 16]
+
+    def weave_out(ap):
+        return ap.rearrange("p (c i t) -> p c t i", i=4, t=PACK)
+
+    def weave_in(ap):
+        return ap.rearrange("p t (c i) -> p c t i", i=4)
+
+    with ExitStack() as ctx:
+        lists = ctx.enter_context(tc.tile_pool(name="lists", bufs=1))
+        keep = ctx.enter_context(tc.tile_pool(name="keep", bufs=1))
+        psum = ctx.enter_context(tc.psum_pool(name="psum", bufs=1))
+
+        def sb(name, width, dtype):
+            return keep.tile([P, width], dtype, name=name, align_bytes=64)
+
+        offs_sb = lists.tile([P, S // 16], U16, name="offs_sb")
+        kq_sb = lists.tile([P, H // 16], U16, name="kq_sb")
+        rt_sb = lists.tile([P, S // 16], U16, name="rt_sb")
+        lf_sb = lists.tile([P, S // 16], U16, name="lf_sb")
+
+        x_word_table = sb("x_word_table", T, U32)
+        x_byte_table = sb("x_byte_table", T, U8)
+        d_byte_table = keep.tile([P, G], U8, name="d_byte_table", tag="d_table", align_bytes=64)
+        w_words_raw = sb("w_words_raw", H, U32)
+        w_bytes_raw = sb("w_bytes_raw", H, U8)
+        d_plane = sb("d_plane", H, U8)
+        gs_sb = sb("gs_sb", PACK, F32)
+        gs_neg = sb("gs_neg", PACK, F32)
+
+        nc.vector.memset(d_byte_table[:].bitcast(I32), 0)
+        nc.vector.memset(x_byte_table[:].bitcast(I32), 0)
+        nc.vector.memset(w_bytes_raw[:].bitcast(I32), 0)
+        nc.gpsimd.memset(d_plane[:].bitcast(I32), 0)
+
+        nc.sync.dma_start(kq_sb[:], kq)
+        nc.sync.dma_start(offs_sb[:], offs)
+        nc.sync.dma_start(rt_sb[:], rt)
+        nc.sync.dma_start(lf_sb[:], lf)
+        nc.sync.dma_start(gs_sb[:], gs.rearrange("(p t) o -> p (t o)", t=PACK))
+        nc.sync.dma_start(x_word_table[:].bitcast(I32), as_words(x_words))
+        nc.sync.dma_start(w_words_raw[:].bitcast(I32), as_words(w1_words))
+        nc.scalar.dma_start(d_byte_table[:].bitcast(I32)[0:P:8, :], d_scales[0].bitcast(I32))
+        for q in range(4):
+            nc.scalar.dma_start(x_byte_table[32 * q : 32 * q + 4, :].bitcast(I32), x_scales[0, 4 * q : 4 * q + 4, :].bitcast(I32))
+        for q in range(4):
+            nc.sync.dma_start(w_bytes_raw[32 * q : 32 * q + 4, :].bitcast(I32), w1_scales[0, 4 * q : 4 * q + 4, :].bitcast(I32))
+
+        x_codes = sb("x_codes", S, U32)
+        x_plane = sb("x_plane", S, U8)
+        w_codes = sb("w_codes", H, U32)
+        w_plane = sb("w_plane", H, U8)
+        d_picked_words = sb("d_picked_words", H, U32)
+        d_picked_bytes = sb("d_picked_bytes", H, U8)
+        d_codes = sb("d_codes", H, U32)
+        d_dealt_bytes = sb("d_dealt_bytes", H, U8)
+
+        nc.vector.tensor_copy(d_picked_bytes[:], d_byte_table[:].indirect(kq_sb[:]))
+        d_word_table = keep.tile([P, G], U32, name="d_word_table", tag="d_table", align_bytes=64)
+        nc.sync.dma_start(d_word_table[:].bitcast(I32), as_words(d_words))
+        nc.vector.tensor_copy(x_plane[:], x_byte_table[:].indirect(offs_sb[:]))
+        nc.vector.tensor_copy(x_codes[:], x_word_table[:].indirect(offs_sb[:]))
+        nc.vector.tensor_copy(planes(w_codes[:].bitcast(I32)), dealt(w_words_raw[:].bitcast(I32)))
+        nc.vector.tensor_copy(planes(w_plane[:]), dealt(w_bytes_raw[:]))
+
+        y = [psum.tile([P, S], F32, name=f"y{t}") for t in range(PACK)]
+        for t in range(PACK):
+            cols = slice(P * t, P * (t + 1))
+            nc.tensor.matmul_mx(
+                y[t][:], lhsT=w_codes[:, cols].bitcast(FP8X4), lhsT_scale=w_plane[:, cols],
+                rhs=x_codes[:].bitcast(FP8X4), rhs_scale=x_plane[:], start=True, stop=True,
+            )
+
+        nc.vector.tensor_copy(planes(d_dealt_bytes[:]), dealt(d_picked_bytes[:]))
+        nc.vector.tensor_copy(d_picked_words[:], d_word_table[:].indirect(kq_sb[:]))
+        for r in range(4):
+            nc.sync.dma_start(d_plane[r:P:32, :].bitcast(I32), d_dealt_bytes[8 * r : P : 32, :].bitcast(I32))
+
+        nc.scalar.activation(gs_neg[:], gs_sb[:], ACT.Copy, scale=-1.0)
+
+        sq = [sb(f"sq{t}", S, F32) for t in range(PACK)]
+        there = [sb(f"there{t}", S, F32) for t in range(PACK)]
+        here = [sb(f"here{t}", S, F32) for t in range(PACK)]
+        uh = [sb(f"uh{t}", S, F32) for t in range(PACK)]
+        flux = [sb(f"flux{t}", S, F32) for t in range(PACK)]
+        flux_window = [sb(f"flux_window{t}", S, F32) for t in range(PACK)]
+        flux_plain = [sb(f"flux_plain{t}", S, F32) for t in range(PACK)]
+
+        for t in range(PACK):
+            nc.scalar.activation(sq[t][:], y[t][:], ACT.Square, scale=0.5)
+
+        def make_there(t):
+            nc.vector.scalar_tensor_tensor(there[t][:], y[t][:], 0.5, sq[t][:], ALU.mult, ALU.subtract)
+
+        def make_here(t):
+            nc.vector.scalar_tensor_tensor(here[t][:], y[t][:], 0.5, sq[t][:], ALU.mult, ALU.add)
+
+        def first_half_step(t):
+            for first in (0, HALF):
+                cols = slice(first, first + HALF)
+                nc.vector.tensor_tensor(uh[t][:, cols], there[t][:].indirect(entries(rt_sb, first, HALF)), here[t][:, cols], ALU.add)
+            nc.scalar.activation(flux[t][:], uh[t][:], ACT.Square, scale=0.5)
+            nc.scalar.activation(flux_window[t][:], flux[t][:], ACT.Copy, scale=gs_neg[:, t : t + 1])
+            nc.scalar.activation(flux_plain[t][:], flux[t][:], ACT.Copy, scale=gs_neg[:, t : t + 1])
+
+        make_there(0)
+        make_here(0)
+        nc.vector.tensor_copy(planes(d_codes[:].bitcast(I32)), dealt(d_picked_words[:].bitcast(I32)))
+        for t in range(PACK):
+            if t + 1 < PACK:
+                make_there(t + 1)
+            first_half_step(t)
+            if t + 1 < PACK:
+                make_here(t + 1)
+
+        out_codes = sb("out_codes", S, U32)
+        out_plane = sb("out_plane", S, U8)
+        out_rows = out_0.rearrange("(p t) j -> p t j", t=PACK)
+        out_words = as_words(out_1)
+
+        z = [keep.tile([P, PACK, PIECE], F32, name=f"z{c}", align_bytes=64) for c in range(PIECES)]
+        z_woven = [sb(f"z_woven{c}", PACK * PIECE, BF16) for c in range(PIECES)]
+        z_codes = [sb(f"z_codes{c}", PIECE, U32) for c in range(PIECES)]
+        z_plane = [sb(f"z_plane{c}", PIECE, U8) for c in range(PIECES)]
+        acc = [psum.tile([P, PACK, PIECE], F32, name=f"acc{c}") for c in range(PIECES)]
+        res = [keep.tile([P, PACK, PIECE], F32, name=f"res{c}", align_bytes=64) for c in range(PIECES)]
+        res_woven = [sb(f"res_woven{c}", PACK * PIECE, BF16) for c in range(PIECES)]
+
+        def second_half_step(c, t):
+            cols = slice(PIECE * c, PIECE * (c + 1))
+            nc.vector.tensor_tensor(
+                z[c][:, t, :], flux_window[t][:].indirect(entries(lf_sb, PIECE * c, PIECE)), flux_plain[t][:, cols], ALU.subtract
+            )
+
+        def weave_z(c):
+            if c + 1 < PIECES:
+                nc.scalar.copy(weave_out(z_woven[c][:]), weave_in(z[c][:]))
+            else:
+                nc.vector.tensor_copy(weave_out(z_woven[c][:]), weave_in(z[c][:]))
+
+        def second_product(c):
+            nc.vector.quantize_mx(z_codes[c][:].bitcast(FP8X4), z_plane[c][:], z_woven[c][:])
+            for t in range(PACK):
+                cols = slice(P * t, P * (t + 1))
+                nc.tensor.matmul_mx(
+                    acc[c][:, t, :], lhsT=d_codes[:, cols].bitcast(FP8X4), lhsT_scale=d_plane[:, cols],
+                    rhs=z_codes[c][:].bitcast(FP8X4), rhs_scale=z_plane[c][:], start=True, stop=True,
+                )
+            nc.scalar.activation(res[c][:], acc[c][:], ACT.Copy, scale=0.0625)
+            nc.sync.dma_start(out_rows[:, :, PIECE * c : PIECE * (c + 1)], res[c][:])
+
+        def weave_result(c):
+            nc.vector.tensor_copy(weave_out(res_woven[c][:]), weave_in(res[c][:]))
+
+        def result_planes(c):
+            cols = slice(PIECE * c, PIECE * (c + 1))
+            nc.vector.quantize_mx(out_codes[:, cols].bitcast(FP8X4), out_plane[:, cols], res_woven[c][:])
+            nc.sync.dma_start(out_words[:, cols], out_codes[:, cols].bitcast(I32))
+
+        for c in (0, 1):
+            for t in range(PACK - 1):
+                second_half_step(c, t)
+        for c in (0, 1):
+            second_half_step(c, PACK - 1)
+            weave_z(c)
+        for t in range(PACK):
+            second_half_step(2, t)
+        weave_z(2)
+        second_product(0)
+        for t in range(PACK):
+            second_half_step(3, t)
+        second_product(1)
+        weave_z(3)
+        second_product(2)
+        weave_result(0)
+        second_product(3)
+        result_planes(0)
+        weave_result(1)
+        weave_result(2)
+        result_planes(1)
+        weave_result(3)
+        result_planes(2)
+        result_planes(3)
+        for q in range(4):
+            queue = nc.sync if q % 2 == 0 else nc.scalar
+            queue.dma_start(out_2[0, 4 * q : 4 * q + 4, :].bitcast(I32), out_plane[32 * q : 32 * q + 4, :].bitcast(I32))

@@ -50,8 +50,8 @@ def tile_picked_wendroff_none_po_kernel(
         keep = ctx.enter_context(tc.tile_pool(name="keep", bufs=1))
         psum = ctx.enter_context(tc.psum_pool(name="psum", bufs=1))
 
-        def sb(name, width, dtype):
-            return keep.tile([P, width], dtype, name=name, align_bytes=64)
+        def sb(name, width, dtype, tag=None):
+            return keep.tile([P, width], dtype, name=name, tag=tag or name, align_bytes=64)
 
         offs_sb = lists.tile([P, S // 16], U16, name="offs_sb")
         kq_sb = lists.tile([P, H // 16], U16, name="kq_sb")
@@ -60,30 +60,31 @@ def tile_picked_wendroff_none_po_kernel(
 
         x_word_table = sb("x_word_table", T, U32)
         x_byte_table = sb("x_byte_table", T, U8)
-        d_byte_table = keep.tile([P, G], U8, name="d_byte_table", tag="d_table", align_bytes=64)
+        d_byte_table = sb("d_byte_table", G, U8)
+        d_word_table = sb("d_word_table", G, U32)
         w_words_raw = sb("w_words_raw", H, U32)
         w_bytes_raw = sb("w_bytes_raw", H, U8)
         d_plane = sb("d_plane", H, U8)
         gs_sb = sb("gs_sb", PACK, F32)
         gs_neg = sb("gs_neg", PACK, F32)
 
-        nc.vector.memset(d_byte_table[:].bitcast(I32), 0)
-        nc.vector.memset(x_byte_table[:].bitcast(I32), 0)
         nc.vector.memset(w_bytes_raw[:].bitcast(I32), 0)
         nc.gpsimd.memset(d_plane[:].bitcast(I32), 0)
 
         nc.sync.dma_start(kq_sb[:], kq)
+        nc.sync.dma_start(d_byte_table[:].bitcast(I32), d_scales[0].bitcast(I32).unsqueeze(1).broadcast_to([16, 8, G // 4]))
         nc.sync.dma_start(offs_sb[:], offs)
+        for q in range(4):
+            rows = x_scales[0, 4 * q : 4 * q + 4, :].bitcast(I32)
+            nc.sync.dma_start(x_byte_table[32 * q : 32 * q + 32, :].bitcast(I32), rows.unsqueeze(0).broadcast_to([8, 4, T // 4]))
+        nc.sync.dma_start(x_word_table[:].bitcast(I32), as_words(x_words))
+        nc.sync.dma_start(w_words_raw[:].bitcast(I32), as_words(w1_words))
+        for q in range(4):
+            nc.sync.dma_start(w_bytes_raw[32 * q : 32 * q + 4, :].bitcast(I32), w1_scales[0, 4 * q : 4 * q + 4, :].bitcast(I32))
+        nc.sync.dma_start(d_word_table[:].bitcast(I32), as_words(d_words))
         nc.sync.dma_start(rt_sb[:], rt)
         nc.sync.dma_start(lf_sb[:], lf)
         nc.sync.dma_start(gs_sb[:], gs.rearrange("(p t) o -> p (t o)", t=PACK))
-        nc.sync.dma_start(x_word_table[:].bitcast(I32), as_words(x_words))
-        nc.sync.dma_start(w_words_raw[:].bitcast(I32), as_words(w1_words))
-        nc.scalar.dma_start(d_byte_table[:].bitcast(I32)[0:P:8, :], d_scales[0].bitcast(I32))
-        for q in range(4):
-            nc.scalar.dma_start(x_byte_table[32 * q : 32 * q + 4, :].bitcast(I32), x_scales[0, 4 * q : 4 * q + 4, :].bitcast(I32))
-        for q in range(4):
-            nc.sync.dma_start(w_bytes_raw[32 * q : 32 * q + 4, :].bitcast(I32), w1_scales[0, 4 * q : 4 * q + 4, :].bitcast(I32))
 
         x_codes = sb("x_codes", S, U32)
         x_plane = sb("x_plane", S, U8)
@@ -95,12 +96,11 @@ def tile_picked_wendroff_none_po_kernel(
         d_dealt_bytes = sb("d_dealt_bytes", H, U8)
 
         nc.vector.tensor_copy(d_picked_bytes[:], d_byte_table[:].indirect(kq_sb[:]))
-        d_word_table = keep.tile([P, G], U32, name="d_word_table", tag="d_table", align_bytes=64)
-        nc.sync.dma_start(d_word_table[:].bitcast(I32), as_words(d_words))
         nc.vector.tensor_copy(x_plane[:], x_byte_table[:].indirect(offs_sb[:]))
         nc.vector.tensor_copy(x_codes[:], x_word_table[:].indirect(offs_sb[:]))
         nc.vector.tensor_copy(planes(w_codes[:].bitcast(I32)), dealt(w_words_raw[:].bitcast(I32)))
         nc.vector.tensor_copy(planes(w_plane[:]), dealt(w_bytes_raw[:]))
+        nc.vector.tensor_copy(planes(d_dealt_bytes[:]), dealt(d_picked_bytes[:]))
 
         y = [psum.tile([P, S], F32, name=f"y{t}") for t in range(PACK)]
         for t in range(PACK):
@@ -110,15 +110,15 @@ def tile_picked_wendroff_none_po_kernel(
                 rhs=x_codes[:].bitcast(FP8X4), rhs_scale=x_plane[:], start=True, stop=True,
             )
 
-        nc.vector.tensor_copy(planes(d_dealt_bytes[:]), dealt(d_picked_bytes[:]))
         nc.vector.tensor_copy(d_picked_words[:], d_word_table[:].indirect(kq_sb[:]))
         for r in range(4):
             nc.sync.dma_start(d_plane[r:P:32, :].bitcast(I32), d_dealt_bytes[8 * r : P : 32, :].bitcast(I32))
 
         nc.scalar.activation(gs_neg[:], gs_sb[:], ACT.Copy, scale=-1.0)
 
-        sq = [sb(f"sq{t}", S, F32) for t in range(PACK)]
-        there = [sb(f"there{t}", S, F32) for t in range(PACK)]
+        right = [sb(f"right{t}", 2 * S, F32) for t in range(PACK)]
+        there = [right[t][:, :S] for t in range(PACK)]
+        sq = [right[t][:, S:] for t in range(PACK)]
         here = [sb(f"here{t}", S, F32) for t in range(PACK)]
         uh = [sb(f"uh{t}", S, F32) for t in range(PACK)]
         flux = [sb(f"flux{t}", S, F32) for t in range(PACK)]
@@ -126,21 +126,20 @@ def tile_picked_wendroff_none_po_kernel(
         flux_plain = [sb(f"flux_plain{t}", S, F32) for t in range(PACK)]
 
         for t in range(PACK):
-            nc.scalar.activation(sq[t][:], y[t][:], ACT.Square, scale=0.5)
+            nc.scalar.activation(sq[t], y[t][:], ACT.Square, scale=0.5)
 
         def make_there(t):
-            nc.vector.scalar_tensor_tensor(there[t][:], y[t][:], 0.5, sq[t][:], ALU.mult, ALU.subtract)
+            nc.vector.scalar_tensor_tensor(there[t], y[t][:], 0.5, sq[t], ALU.mult, ALU.subtract)
 
         def make_here(t):
-            nc.vector.scalar_tensor_tensor(here[t][:], y[t][:], 0.5, sq[t][:], ALU.mult, ALU.add)
+            nc.vector.scalar_tensor_tensor(here[t][:], y[t][:], 0.5, sq[t], ALU.mult, ALU.add)
 
         def first_half_step(t):
-            for first in (0, HALF):
-                cols = slice(first, first + HALF)
-                nc.vector.tensor_tensor(uh[t][:, cols], there[t][:].indirect(entries(rt_sb, first, HALF)), here[t][:, cols], ALU.add)
+            nc.vector.tensor_tensor(uh[t][:], right[t][:].indirect(rt_sb[:]), here[t][:], ALU.add)
             nc.scalar.activation(flux[t][:], uh[t][:], ACT.Square, scale=0.5)
             nc.scalar.activation(flux_window[t][:], flux[t][:], ACT.Copy, scale=gs_neg[:, t : t + 1])
-            nc.scalar.activation(flux_plain[t][:], flux[t][:], ACT.Copy, scale=gs_neg[:, t : t + 1])
+            for cols in [slice(0, S)] if t + 1 < PACK else [slice(0, HALF), slice(HALF, S)]:
+                nc.scalar.activation(flux_plain[t][:, cols], flux[t][:, cols], ACT.Copy, scale=gs_neg[:, t : t + 1])
 
         make_there(0)
         make_here(0)
@@ -157,69 +156,79 @@ def tile_picked_wendroff_none_po_kernel(
         out_rows = out_0.rearrange("(p t) j -> p t j", t=PACK)
         out_words = as_words(out_1)
 
-        z = [keep.tile([P, PACK, PIECE], F32, name=f"z{c}", align_bytes=64) for c in range(PIECES)]
-        z_woven = [sb(f"z_woven{c}", PACK * PIECE, BF16) for c in range(PIECES)]
-        z_codes = [sb(f"z_codes{c}", PIECE, U32) for c in range(PIECES)]
-        z_plane = [sb(f"z_plane{c}", PIECE, U8) for c in range(PIECES)]
-        acc = [psum.tile([P, PACK, PIECE], F32, name=f"acc{c}") for c in range(PIECES)]
-        res = [keep.tile([P, PACK, PIECE], F32, name=f"res{c}", align_bytes=64) for c in range(PIECES)]
-        res_woven = [sb(f"res_woven{c}", PACK * PIECE, BF16) for c in range(PIECES)]
+        widths = [128, 128, 128, 128]
+        starts = [0, 128, 256, 384]
+        pieces = range(len(widths))
+        z = {}
+        z_woven = [sb(f"z_woven{c}", PACK * widths[c], BF16) for c in pieces]
+        z_tags = ["z0", "z1", "flux3", "z_woven0"]
+        z_codes = [sb(f"z_codes{c}", widths[c], U32) for c in pieces]
+        z_plane = [sb(f"z_plane{c}", widths[c], U8) for c in pieces]
+        res = [keep.tile([P, PACK, widths[c]], F32, name=f"res{c}", align_bytes=64) for c in pieces]
+        res_woven = [sb(f"res_woven{c}", PACK * widths[c], BF16) for c in pieces]
+        acc = {}
+
+        def span(c):
+            return slice(starts[c], starts[c] + widths[c])
 
         def second_half_step(c, t):
-            cols = slice(PIECE * c, PIECE * (c + 1))
+            if t == 0:
+                z[c] = keep.tile([P, PACK, widths[c]], F32, name=f"z{c}", tag=z_tags[c], align_bytes=64)
             nc.vector.tensor_tensor(
-                z[c][:, t, :], flux_window[t][:].indirect(entries(lf_sb, PIECE * c, PIECE)), flux_plain[t][:, cols], ALU.subtract
+                z[c][:, t, :], flux_window[t][:].indirect(entries(lf_sb, starts[c], widths[c])), flux_plain[t][:, span(c)], ALU.subtract
             )
-
-        def weave_z(c):
-            if c + 1 < PIECES:
-                nc.scalar.copy(weave_out(z_woven[c][:]), weave_in(z[c][:]))
-            else:
-                nc.vector.tensor_copy(weave_out(z_woven[c][:]), weave_in(z[c][:]))
 
         def second_product(c):
             nc.vector.quantize_mx(z_codes[c][:].bitcast(FP8X4), z_plane[c][:], z_woven[c][:])
-            for t in range(PACK):
-                cols = slice(P * t, P * (t + 1))
-                nc.tensor.matmul_mx(
-                    acc[c][:, t, :], lhsT=d_codes[:, cols].bitcast(FP8X4), lhsT_scale=d_plane[:, cols],
-                    rhs=z_codes[c][:].bitcast(FP8X4), rhs_scale=z_plane[c][:], start=True, stop=True,
-                )
-            nc.scalar.activation(res[c][:], acc[c][:], ACT.Copy, scale=0.0625)
-            nc.sync.dma_start(out_rows[:, :, PIECE * c : PIECE * (c + 1)], res[c][:])
+            per_bank = S // widths[c]
+            for b in range(PACK // per_bank):
+                bank = psum.tile([P, per_bank, widths[c]], F32, name=f"acc{c}_{b}")
+                acc[c, b] = bank
+                for u in range(per_bank):
+                    t = b * per_bank + u
+                    cols = slice(P * t, P * (t + 1))
+                    nc.tensor.matmul_mx(
+                        bank[:, u, :], lhsT=d_codes[:, cols].bitcast(FP8X4), lhsT_scale=d_plane[:, cols],
+                        rhs=z_codes[c][:].bitcast(FP8X4), rhs_scale=z_plane[c][:], start=True, stop=True,
+                    )
 
-        def weave_result(c):
-            nc.vector.tensor_copy(weave_out(res_woven[c][:]), weave_in(res[c][:]))
+        def store_result(c):
+            per_bank = S // widths[c]
+            for b in range(PACK // per_bank):
+                nc.scalar.activation(res[c][:, b * per_bank : (b + 1) * per_bank, :], acc[c, b][:], ACT.Copy, scale=0.0625)
+            nc.sync.dma_start(out_rows[:, :, span(c)], res[c][:])
 
         def result_planes(c):
-            cols = slice(PIECE * c, PIECE * (c + 1))
-            nc.vector.quantize_mx(out_codes[:, cols].bitcast(FP8X4), out_plane[:, cols], res_woven[c][:])
-            nc.sync.dma_start(out_words[:, cols], out_codes[:, cols].bitcast(I32))
+            nc.vector.quantize_mx(out_codes[:, span(c)].bitcast(FP8X4), out_plane[:, span(c)], res_woven[c][:])
+            nc.sync.dma_start(out_words[:, span(c)], out_codes[:, span(c)].bitcast(I32))
 
         for c in (0, 1):
             for t in range(PACK - 1):
                 second_half_step(c, t)
         for c in (0, 1):
             second_half_step(c, PACK - 1)
-            weave_z(c)
+            nc.scalar.copy(weave_out(z_woven[c][:]), weave_in(z[c][:]))
         for t in range(PACK):
             second_half_step(2, t)
-        weave_z(2)
-        second_product(0)
+        nc.scalar.copy(weave_out(z_woven[2][:]), weave_in(z[2][:]))
+        for c in (0, 1):
+            second_product(c)
+            store_result(c)
         for t in range(PACK):
             second_half_step(3, t)
-        second_product(1)
-        weave_z(3)
         second_product(2)
-        weave_result(0)
+        nc.vector.tensor_copy(weave_out(z_woven[3][:]), weave_in(z[3][:]))
+        nc.scalar.copy(weave_out(res_woven[0][:]), weave_in(res[0][:]))
         second_product(3)
+        store_result(2)
+        nc.scalar.copy(weave_out(res_woven[1][:]), weave_in(res[1][:]))
         result_planes(0)
-        weave_result(1)
-        weave_result(2)
-        result_planes(1)
-        weave_result(3)
-        result_planes(2)
+        nc.vector.tensor_scalar(weave_out(res_woven[3][:]), weave_in(acc[3, 0][:]), 0.0625, None, ALU.mult)
+        store_result(3)
+        nc.vector.tensor_copy(weave_out(res_woven[2][:]), weave_in(res[2][:]))
         result_planes(3)
+        result_planes(1)
+        result_planes(2)
         for q in range(4):
             queue = nc.sync if q % 2 == 0 else nc.scalar
             queue.dma_start(out_2[0, 4 * q : 4 * q + 4, :].bitcast(I32), out_plane[32 * q : 32 * q + 4, :].bitcast(I32))

@@ -17,7 +17,6 @@ ACT = mybir.ActivationFunctionType
 
 P = 128
 PACK = 4
-HALF = S // 2
 PIECE = 128
 PIECES = S // PIECE
 
@@ -30,11 +29,10 @@ def tile_picked_wendroff_none_po_kernel(
     def as_words(dram):
         return dram[0].rearrange("p n t -> p (n t)").bitcast(I32)
 
-    def dealt(ap):
-        return ap.rearrange("p (m t) -> p t m", t=PACK)
-
-    def planes(ap):
-        return ap.rearrange("p (t m) -> p t m", t=PACK)
+    def deal(dst, src, run):
+        nc.vector.tensor_copy(
+            dst.rearrange("p (t c i) -> p c t i", t=PACK, i=run), src.rearrange("p (c i t) -> p c t i", t=PACK, i=run)
+        )
 
     def entries(offsets, first, count):
         return offsets[:, first // 16 : (first + count) // 16]
@@ -59,50 +57,47 @@ def tile_picked_wendroff_none_po_kernel(
         lf_sb = lists.tile([P, S // 16], U16, name="lf_sb")
 
         x_word_table = sb("x_word_table", T, U32)
-        x_byte_table = sb("x_byte_table", T, U8)
+        x_byte_table = sb("x_byte_table", T, U8, tag="table")
         d_byte_table = sb("d_byte_table", G, U8)
-        d_word_table = sb("d_word_table", G, U32)
         w_words_raw = sb("w_words_raw", H, U32)
-        w_bytes_raw = sb("w_bytes_raw", H, U8)
+        w_bytes_raw = sb("w_bytes_raw", H, U8, tag="bytes_to_deal")
         d_plane = sb("d_plane", H, U8)
         gs_sb = sb("gs_sb", PACK, F32)
         gs_neg = sb("gs_neg", PACK, F32)
 
-        nc.vector.memset(w_bytes_raw[:].bitcast(I32), 0)
-        nc.gpsimd.memset(d_plane[:].bitcast(I32), 0)
+        for tile in (d_plane, x_byte_table, w_bytes_raw, d_byte_table):
+            nc.vector.memset(tile[:].bitcast(I32), 0)
 
-        nc.sync.dma_start(kq_sb[:], kq)
-        nc.sync.dma_start(d_byte_table[:].bitcast(I32), d_scales[0].bitcast(I32).unsqueeze(1).broadcast_to([16, 8, G // 4]))
-        nc.sync.dma_start(offs_sb[:], offs)
-        for q in range(4):
-            rows = x_scales[0, 4 * q : 4 * q + 4, :].bitcast(I32)
-            nc.sync.dma_start(x_byte_table[32 * q : 32 * q + 32, :].bitcast(I32), rows.unsqueeze(0).broadcast_to([8, 4, T // 4]))
+        def load_scale_rows(queue, tile, dram):
+            for q in range(4):
+                queue.dma_start(tile[32 * q : 32 * q + 4, :].bitcast(I32), dram[0, 4 * q : 4 * q + 4, :].bitcast(I32))
+
+        for tile, dram in ((offs_sb, offs), (kq_sb, kq), (rt_sb, rt), (lf_sb, lf)):
+            nc.sync.dma_start(tile[:], dram)
         nc.sync.dma_start(x_word_table[:].bitcast(I32), as_words(x_words))
         nc.sync.dma_start(w_words_raw[:].bitcast(I32), as_words(w1_words))
-        for q in range(4):
-            nc.sync.dma_start(w_bytes_raw[32 * q : 32 * q + 4, :].bitcast(I32), w1_scales[0, 4 * q : 4 * q + 4, :].bitcast(I32))
-        nc.sync.dma_start(d_word_table[:].bitcast(I32), as_words(d_words))
-        nc.sync.dma_start(rt_sb[:], rt)
-        nc.sync.dma_start(lf_sb[:], lf)
-        nc.sync.dma_start(gs_sb[:], gs.rearrange("(p t) o -> p (t o)", t=PACK))
+        load_scale_rows(nc.scalar, x_byte_table, x_scales)
+        load_scale_rows(nc.scalar, w_bytes_raw, w1_scales)
+        nc.scalar.dma_start(d_byte_table[:].bitcast(I32)[0:P:8, :], d_scales[0].bitcast(I32))
+        nc.gpsimd.dma_start(gs_sb[:], gs.rearrange("(p t) o -> p (t o)", t=PACK))
+        nc.gpsimd.tensor_scalar(gs_neg[:], gs_sb[:], -1.0, 0.0, ALU.mult, ALU.add)
 
         x_codes = sb("x_codes", S, U32)
         x_plane = sb("x_plane", S, U8)
         w_codes = sb("w_codes", H, U32)
         w_plane = sb("w_plane", H, U8)
-        d_picked_words = sb("d_picked_words", H, U32)
-        d_picked_bytes = sb("d_picked_bytes", H, U8)
         d_codes = sb("d_codes", H, U32)
         d_dealt_bytes = sb("d_dealt_bytes", H, U8)
 
-        nc.vector.tensor_copy(d_picked_bytes[:], d_byte_table[:].indirect(kq_sb[:]))
-        nc.vector.tensor_copy(x_plane[:], x_byte_table[:].indirect(offs_sb[:]))
         nc.vector.tensor_copy(x_codes[:], x_word_table[:].indirect(offs_sb[:]))
-        nc.vector.tensor_copy(planes(w_codes[:].bitcast(I32)), dealt(w_words_raw[:].bitcast(I32)))
-        nc.vector.tensor_copy(planes(w_plane[:]), dealt(w_bytes_raw[:]))
-        nc.vector.tensor_copy(planes(d_dealt_bytes[:]), dealt(d_picked_bytes[:]))
+        deal(w_codes[:].bitcast(I32), w_words_raw[:].bitcast(I32), 4)
+        nc.vector.tensor_copy(x_plane[:], x_byte_table[:].indirect(offs_sb[:]))
+        deal(w_plane[:], w_bytes_raw[:], 16)
 
-        y = [psum.tile([P, S], F32, name=f"y{t}") for t in range(PACK)]
+        d_word_table = sb("d_word_table", G, U32, tag="table")
+        nc.sync.dma_start(d_word_table[:].bitcast(I32), as_words(d_words))
+
+        y = [psum.tile([P, S], F32, name=f"y{t}", tag=f"y{t}") for t in range(PACK)]
         for t in range(PACK):
             cols = slice(P * t, P * (t + 1))
             nc.tensor.matmul_mx(
@@ -110,11 +105,11 @@ def tile_picked_wendroff_none_po_kernel(
                 rhs=x_codes[:].bitcast(FP8X4), rhs_scale=x_plane[:], start=True, stop=True,
             )
 
-        nc.vector.tensor_copy(d_picked_words[:], d_word_table[:].indirect(kq_sb[:]))
+        d_picked_bytes = sb("d_picked_bytes", H, U8, tag="bytes_to_deal")
+        nc.vector.tensor_copy(d_picked_bytes[:], d_byte_table[:].indirect(kq_sb[:]))
+        deal(d_dealt_bytes[:], d_picked_bytes[:], 16)
         for r in range(4):
             nc.sync.dma_start(d_plane[r:P:32, :].bitcast(I32), d_dealt_bytes[8 * r : P : 32, :].bitcast(I32))
-
-        nc.scalar.activation(gs_neg[:], gs_sb[:], ACT.Copy, scale=-1.0)
 
         right = [sb(f"right{t}", 2 * S, F32) for t in range(PACK)]
         there = [right[t][:, :S] for t in range(PACK)]
@@ -138,12 +133,10 @@ def tile_picked_wendroff_none_po_kernel(
             nc.vector.tensor_tensor(uh[t][:], right[t][:].indirect(rt_sb[:]), here[t][:], ALU.add)
             nc.scalar.activation(flux[t][:], uh[t][:], ACT.Square, scale=0.5)
             nc.scalar.activation(flux_window[t][:], flux[t][:], ACT.Copy, scale=gs_neg[:, t : t + 1])
-            for cols in [slice(0, S)] if t + 1 < PACK else [slice(0, HALF), slice(HALF, S)]:
-                nc.scalar.activation(flux_plain[t][:, cols], flux[t][:, cols], ACT.Copy, scale=gs_neg[:, t : t + 1])
+            nc.scalar.activation(flux_plain[t][:], flux[t][:], ACT.Copy, scale=gs_neg[:, t : t + 1])
 
         make_there(0)
         make_here(0)
-        nc.vector.tensor_copy(planes(d_codes[:].bitcast(I32)), dealt(d_picked_words[:].bitcast(I32)))
         for t in range(PACK):
             if t + 1 < PACK:
                 make_there(t + 1)
@@ -151,84 +144,79 @@ def tile_picked_wendroff_none_po_kernel(
             if t + 1 < PACK:
                 make_here(t + 1)
 
+        d_picked_words = sb("d_picked_words", H, U32, tag=f"right{PACK - 1}")
+        nc.vector.tensor_copy(d_picked_words[:], d_word_table[:].indirect(kq_sb[:]))
+        deal(d_codes[:].bitcast(I32), d_picked_words[:].bitcast(I32), 4)
+
         out_codes = sb("out_codes", S, U32)
         out_plane = sb("out_plane", S, U8)
         out_rows = out_0.rearrange("(p t) j -> p t j", t=PACK)
         out_words = as_words(out_1)
 
-        widths = [128, 128, 128, 128]
-        starts = [0, 128, 256, 384]
-        pieces = range(len(widths))
+        last = PIECES - 1
+        z_woven = [sb(f"z_woven{c}", PACK * PIECE, BF16) for c in range(PIECES)]
+        z_codes = [sb(f"z_codes{c}", PIECE, U32) for c in range(PIECES)]
+        z_plane = [sb(f"z_plane{c}", PIECE, U8) for c in range(PIECES)]
+        res = [keep.tile([P, PACK, PIECE], F32, name=f"res{c}", align_bytes=64) for c in range(PIECES)]
+        res_woven = [sb(f"res_woven{c}", PACK * PIECE, BF16) for c in range(PIECES)]
         z = {}
-        z_woven = [sb(f"z_woven{c}", PACK * widths[c], BF16) for c in pieces]
-        z_tags = ["z0", "z1", "flux3", "z_woven0"]
-        z_codes = [sb(f"z_codes{c}", widths[c], U32) for c in pieces]
-        z_plane = [sb(f"z_plane{c}", widths[c], U8) for c in pieces]
-        res = [keep.tile([P, PACK, widths[c]], F32, name=f"res{c}", align_bytes=64) for c in pieces]
-        res_woven = [sb(f"res_woven{c}", PACK * widths[c], BF16) for c in pieces]
-        acc = {}
+        banks = {}
 
         def span(c):
-            return slice(starts[c], starts[c] + widths[c])
+            return slice(PIECE * c, PIECE * (c + 1))
 
-        def second_half_step(c, t):
-            if t == 0:
-                z[c] = keep.tile([P, PACK, widths[c]], F32, name=f"z{c}", tag=z_tags[c], align_bytes=64)
-            nc.vector.tensor_tensor(
-                z[c][:, t, :], flux_window[t][:].indirect(entries(lf_sb, starts[c], widths[c])), flux_plain[t][:, span(c)], ALU.subtract
-            )
+        def second_half_step(c):
+            z[c] = keep.tile([P, PACK, PIECE], F32, name=f"z{c}", tag=f"z{c}" if c < 2 else f"z_woven{c - 2}", align_bytes=64)
+            for t in range(PACK):
+                nc.vector.tensor_tensor(
+                    z[c][:, t, :], flux_window[t][:].indirect(entries(lf_sb, PIECE * c, PIECE)), flux_plain[t][:, span(c)], ALU.subtract
+                )
 
         def second_product(c):
             nc.vector.quantize_mx(z_codes[c][:].bitcast(FP8X4), z_plane[c][:], z_woven[c][:])
-            per_bank = S // widths[c]
-            for b in range(PACK // per_bank):
-                bank = psum.tile([P, per_bank, widths[c]], F32, name=f"acc{c}_{b}")
-                acc[c, b] = bank
-                for u in range(per_bank):
-                    t = b * per_bank + u
-                    cols = slice(P * t, P * (t + 1))
-                    nc.tensor.matmul_mx(
-                        bank[:, u, :], lhsT=d_codes[:, cols].bitcast(FP8X4), lhsT_scale=d_plane[:, cols],
-                        rhs=z_codes[c][:].bitcast(FP8X4), rhs_scale=z_plane[c][:], start=True, stop=True,
-                    )
+            count = 2 if c == last else 1
+            per_bank = PACK // count
+            banks[c] = [psum.tile([P, per_bank, PIECE], F32, name=f"acc{c}_{b}", tag=f"acc{c}" if b == 0 else "y0") for b in range(count)]
+            for t in range(PACK):
+                cols = slice(P * t, P * (t + 1))
+                nc.tensor.matmul_mx(
+                    banks[c][t // per_bank][:, t % per_bank, :], lhsT=d_codes[:, cols].bitcast(FP8X4), lhsT_scale=d_plane[:, cols],
+                    rhs=z_codes[c][:].bitcast(FP8X4), rhs_scale=z_plane[c][:], start=True, stop=True,
+                )
 
         def store_result(c):
-            per_bank = S // widths[c]
-            for b in range(PACK // per_bank):
-                nc.scalar.activation(res[c][:, b * per_bank : (b + 1) * per_bank, :], acc[c, b][:], ACT.Copy, scale=0.0625)
+            per_bank = PACK // len(banks[c])
+            for b, bank in enumerate(banks[c]):
+                nc.scalar.activation(res[c][:, b * per_bank : (b + 1) * per_bank, :], bank[:], ACT.Copy, scale=0.0625)
             nc.sync.dma_start(out_rows[:, :, span(c)], res[c][:])
 
-        def result_planes(c):
-            nc.vector.quantize_mx(out_codes[:, span(c)].bitcast(FP8X4), out_plane[:, span(c)], res_woven[c][:])
-            nc.sync.dma_start(out_words[:, span(c)], out_codes[:, span(c)].bitcast(I32))
+        def weave_from_bank(c):
+            nc.scalar.activation(
+                res_woven[c][:].rearrange("p (n t) -> p n t", t=PACK), banks[c][0][:].rearrange("p t n -> p n t"), ACT.Copy, scale=0.0625
+            )
 
-        for c in (0, 1):
-            for t in range(PACK - 1):
-                second_half_step(c, t)
-        for c in (0, 1):
-            second_half_step(c, PACK - 1)
-            nc.scalar.copy(weave_out(z_woven[c][:]), weave_in(z[c][:]))
-        for t in range(PACK):
-            second_half_step(2, t)
-        nc.scalar.copy(weave_out(z_woven[2][:]), weave_in(z[2][:]))
-        for c in (0, 1):
-            second_product(c)
+        def quantize_result(c):
+            nc.vector.quantize_mx(out_codes[:, span(c)].bitcast(FP8X4), out_plane[:, span(c)], res_woven[c][:])
+
+        second_half_step(0)
+        nc.scalar.copy(weave_out(z_woven[0][:]), weave_in(z[0][:]))
+        for c in range(1, PIECES):
+            second_half_step(c)
+            second_product(c - 1)
+            if c < last:
+                nc.scalar.copy(weave_out(z_woven[c][:]), weave_in(z[c][:]))
+        nc.vector.tensor_copy(weave_out(z_woven[last][:]), weave_in(z[last][:]))
+        second_product(last)
+        for c in range(PIECES):
             store_result(c)
-        for t in range(PACK):
-            second_half_step(3, t)
-        second_product(2)
-        nc.vector.tensor_copy(weave_out(z_woven[3][:]), weave_in(z[3][:]))
-        nc.scalar.copy(weave_out(res_woven[0][:]), weave_in(res[0][:]))
-        second_product(3)
-        store_result(2)
-        nc.scalar.copy(weave_out(res_woven[1][:]), weave_in(res[1][:]))
-        result_planes(0)
-        nc.vector.tensor_scalar(weave_out(res_woven[3][:]), weave_in(acc[3, 0][:]), 0.0625, None, ALU.mult)
-        store_result(3)
-        nc.vector.tensor_copy(weave_out(res_woven[2][:]), weave_in(res[2][:]))
-        result_planes(3)
-        result_planes(1)
-        result_planes(2)
+            if c == 0:
+                weave_from_bank(c)
+            else:
+                nc.vector.tensor_copy(weave_out(res_woven[c][:]), weave_in(res[c][:]))
+            quantize_result(c)
+            if c >= last - 1:
+                cols = slice(0, PIECE * last) if c < last else span(last)
+                nc.sync.dma_start(out_words[:, cols], out_codes[:, cols].bitcast(I32))
         for q in range(4):
-            queue = nc.sync if q % 2 == 0 else nc.scalar
+            queue = nc.scalar if q % 2 == 0 else nc.sync
             queue.dma_start(out_2[0, 4 * q : 4 * q + 4, :].bitcast(I32), out_plane[32 * q : 32 * q + 4, :].bitcast(I32))

@@ -57,45 +57,48 @@ def tile_picked_wendroff_none_po_kernel(
         lf_sb = lists.tile([P, S // 16], U16, name="lf_sb")
 
         x_word_table = sb("x_word_table", T, U32)
-        x_byte_table = sb("x_byte_table", T, U8, tag="table")
+        x_byte_table = sb("x_byte_table", T, U8)
         d_byte_table = sb("d_byte_table", G, U8)
+        d_word_table = sb("d_word_table", G, U32)
         w_words_raw = sb("w_words_raw", H, U32)
-        w_bytes_raw = sb("w_bytes_raw", H, U8, tag="bytes_to_deal")
+        w_bytes_raw = sb("w_bytes_raw", H, U8)
         d_plane = sb("d_plane", H, U8)
         gs_sb = sb("gs_sb", PACK, F32)
         gs_neg = sb("gs_neg", PACK, F32)
 
-        for tile in (d_plane, x_byte_table, w_bytes_raw, d_byte_table):
-            nc.vector.memset(tile[:].bitcast(I32), 0)
+        nc.vector.memset(w_bytes_raw[:].bitcast(I32), 0)
+        nc.gpsimd.memset(d_plane[:].bitcast(I32), 0)
 
-        def load_scale_rows(queue, tile, dram):
-            for q in range(4):
-                queue.dma_start(tile[32 * q : 32 * q + 4, :].bitcast(I32), dram[0, 4 * q : 4 * q + 4, :].bitcast(I32))
-
-        for tile, dram in ((offs_sb, offs), (kq_sb, kq), (rt_sb, rt), (lf_sb, lf)):
-            nc.sync.dma_start(tile[:], dram)
+        nc.sync.dma_start(kq_sb[:], kq)
+        nc.sync.dma_start(d_byte_table[:].bitcast(I32), d_scales[0].bitcast(I32).unsqueeze(1).broadcast_to([16, 8, G // 4]))
+        nc.sync.dma_start(offs_sb[:], offs)
+        for q in range(4):
+            rows = x_scales[0, 4 * q : 4 * q + 4, :].bitcast(I32)
+            nc.sync.dma_start(x_byte_table[32 * q : 32 * q + 32, :].bitcast(I32), rows.unsqueeze(0).broadcast_to([8, 4, T // 4]))
         nc.sync.dma_start(x_word_table[:].bitcast(I32), as_words(x_words))
         nc.sync.dma_start(w_words_raw[:].bitcast(I32), as_words(w1_words))
-        load_scale_rows(nc.scalar, x_byte_table, x_scales)
-        load_scale_rows(nc.scalar, w_bytes_raw, w1_scales)
-        nc.scalar.dma_start(d_byte_table[:].bitcast(I32)[0:P:8, :], d_scales[0].bitcast(I32))
-        nc.gpsimd.dma_start(gs_sb[:], gs.rearrange("(p t) o -> p (t o)", t=PACK))
-        nc.gpsimd.tensor_scalar(gs_neg[:], gs_sb[:], -1.0, 0.0, ALU.mult, ALU.add)
+        for q in range(4):
+            nc.sync.dma_start(w_bytes_raw[32 * q : 32 * q + 4, :].bitcast(I32), w1_scales[0, 4 * q : 4 * q + 4, :].bitcast(I32))
+        nc.sync.dma_start(d_word_table[:].bitcast(I32), as_words(d_words))
+        nc.sync.dma_start(rt_sb[:], rt)
+        nc.sync.dma_start(lf_sb[:], lf)
+        nc.sync.dma_start(gs_sb[:], gs.rearrange("(p t) o -> p (t o)", t=PACK))
 
         x_codes = sb("x_codes", S, U32)
         x_plane = sb("x_plane", S, U8)
         w_codes = sb("w_codes", H, U32)
         w_plane = sb("w_plane", H, U8)
+        d_picked_words = sb("d_picked_words", H, U32)
+        d_picked_bytes = sb("d_picked_bytes", H, U8)
         d_codes = sb("d_codes", H, U32)
         d_dealt_bytes = sb("d_dealt_bytes", H, U8)
 
+        nc.vector.tensor_copy(d_picked_bytes[:], d_byte_table[:].indirect(kq_sb[:]))
+        nc.vector.tensor_copy(x_plane[:], x_byte_table[:].indirect(offs_sb[:]))
         nc.vector.tensor_copy(x_codes[:], x_word_table[:].indirect(offs_sb[:]))
         deal(w_codes[:].bitcast(I32), w_words_raw[:].bitcast(I32), 4)
-        nc.vector.tensor_copy(x_plane[:], x_byte_table[:].indirect(offs_sb[:]))
         deal(w_plane[:], w_bytes_raw[:], 16)
-
-        d_word_table = sb("d_word_table", G, U32, tag="table")
-        nc.sync.dma_start(d_word_table[:].bitcast(I32), as_words(d_words))
+        deal(d_dealt_bytes[:], d_picked_bytes[:], 16)
 
         y = [psum.tile([P, S], F32, name=f"y{t}", tag=f"y{t}") for t in range(PACK)]
         for t in range(PACK):
@@ -105,11 +108,11 @@ def tile_picked_wendroff_none_po_kernel(
                 rhs=x_codes[:].bitcast(FP8X4), rhs_scale=x_plane[:], start=True, stop=True,
             )
 
-        d_picked_bytes = sb("d_picked_bytes", H, U8, tag="bytes_to_deal")
-        nc.vector.tensor_copy(d_picked_bytes[:], d_byte_table[:].indirect(kq_sb[:]))
-        deal(d_dealt_bytes[:], d_picked_bytes[:], 16)
+        nc.vector.tensor_copy(d_picked_words[:], d_word_table[:].indirect(kq_sb[:]))
         for r in range(4):
             nc.sync.dma_start(d_plane[r:P:32, :].bitcast(I32), d_dealt_bytes[8 * r : P : 32, :].bitcast(I32))
+
+        nc.scalar.activation(gs_neg[:], gs_sb[:], ACT.Copy, scale=-1.0)
 
         right = [sb(f"right{t}", 2 * S, F32) for t in range(PACK)]
         there = [right[t][:, :S] for t in range(PACK)]
@@ -133,20 +136,18 @@ def tile_picked_wendroff_none_po_kernel(
             nc.vector.tensor_tensor(uh[t][:], right[t][:].indirect(rt_sb[:]), here[t][:], ALU.add)
             nc.scalar.activation(flux[t][:], uh[t][:], ACT.Square, scale=0.5)
             nc.scalar.activation(flux_window[t][:], flux[t][:], ACT.Copy, scale=gs_neg[:, t : t + 1])
-            nc.scalar.activation(flux_plain[t][:], flux[t][:], ACT.Copy, scale=gs_neg[:, t : t + 1])
+            for cols in [slice(0, S)] if t + 1 < PACK else [slice(0, S // 2), slice(S // 2, S)]:
+                nc.scalar.activation(flux_plain[t][:, cols], flux[t][:, cols], ACT.Copy, scale=gs_neg[:, t : t + 1])
 
         make_there(0)
         make_here(0)
+        deal(d_codes[:].bitcast(I32), d_picked_words[:].bitcast(I32), 4)
         for t in range(PACK):
             if t + 1 < PACK:
                 make_there(t + 1)
             first_half_step(t)
             if t + 1 < PACK:
                 make_here(t + 1)
-
-        d_picked_words = sb("d_picked_words", H, U32, tag=f"right{PACK - 1}")
-        nc.vector.tensor_copy(d_picked_words[:], d_word_table[:].indirect(kq_sb[:]))
-        deal(d_codes[:].bitcast(I32), d_picked_words[:].bitcast(I32), 4)
 
         out_codes = sb("out_codes", S, U32)
         out_plane = sb("out_plane", S, U8)
@@ -165,18 +166,21 @@ def tile_picked_wendroff_none_po_kernel(
         def span(c):
             return slice(PIECE * c, PIECE * (c + 1))
 
-        def second_half_step(c):
-            z[c] = keep.tile([P, PACK, PIECE], F32, name=f"z{c}", tag=f"z{c}" if c < 2 else f"z_woven{c - 2}", align_bytes=64)
-            for t in range(PACK):
+        z_tags = ["z0", "z1", f"flux{PACK - 1}", "z_woven0"]
+
+        def second_half_step(c, planes):
+            for t in planes:
+                if t == 0:
+                    z[c] = keep.tile([P, PACK, PIECE], F32, name=f"z{c}", tag=z_tags[c], align_bytes=64)
                 nc.vector.tensor_tensor(
                     z[c][:, t, :], flux_window[t][:].indirect(entries(lf_sb, PIECE * c, PIECE)), flux_plain[t][:, span(c)], ALU.subtract
                 )
 
         def second_product(c):
             nc.vector.quantize_mx(z_codes[c][:].bitcast(FP8X4), z_plane[c][:], z_woven[c][:])
-            count = 2 if c == last else 1
+            count = PACK if c == last else 1
             per_bank = PACK // count
-            banks[c] = [psum.tile([P, per_bank, PIECE], F32, name=f"acc{c}_{b}", tag=f"acc{c}" if b == 0 else "y0") for b in range(count)]
+            banks[c] = [psum.tile([P, per_bank, PIECE], F32, name=f"acc{c}_{b}", tag=f"acc{c}" if b == 0 else f"y{b}") for b in range(count)]
             for t in range(PACK):
                 cols = slice(P * t, P * (t + 1))
                 nc.tensor.matmul_mx(
@@ -198,13 +202,17 @@ def tile_picked_wendroff_none_po_kernel(
         def quantize_result(c):
             nc.vector.quantize_mx(out_codes[:, span(c)].bitcast(FP8X4), out_plane[:, span(c)], res_woven[c][:])
 
-        second_half_step(0)
-        nc.scalar.copy(weave_out(z_woven[0][:]), weave_in(z[0][:]))
-        for c in range(1, PIECES):
-            second_half_step(c)
-            second_product(c - 1)
-            if c < last:
-                nc.scalar.copy(weave_out(z_woven[c][:]), weave_in(z[c][:]))
+        for c in (0, 1):
+            second_half_step(c, range(PACK - 1))
+        for c in (0, 1):
+            second_half_step(c, [PACK - 1])
+            nc.scalar.copy(weave_out(z_woven[c][:]), weave_in(z[c][:]))
+        second_half_step(2, range(PACK))
+        nc.scalar.copy(weave_out(z_woven[2][:]), weave_in(z[2][:]))
+        second_product(0)
+        second_product(1)
+        second_half_step(last, range(PACK))
+        second_product(2)
         nc.vector.tensor_copy(weave_out(z_woven[last][:]), weave_in(z[last][:]))
         second_product(last)
         for c in range(PIECES):

from contextlib import ExitStack

import concourse.mybir as mybir

K, T, S, H, G = 512, 2048, 512, 512, 2048
FLOPS = 2 * K * H * S * 2

F32 = mybir.dt.float32
BF16 = mybir.dt.bfloat16
I32 = mybir.dt.int32
U32 = mybir.dt.uint32
U16 = mybir.dt.uint16
U8 = mybir.dt.uint8
FP8X4 = mybir.dt.float8_e4m3fn_x4
ALU = mybir.AluOpType
ACT = mybir.ActivationFunctionType

P = 128
PACK = 4
PIECE = 128
PIECES = S // PIECE


def tile_picked_wendroff_none_po_kernel(
    tc, x_words, x_scales, w1_words, w1_scales, gs, d_words, d_scales, offs, rt, lf, kq, out_0, out_1, out_2
):
    nc = tc.nc

    def as_words(dram):
        return dram[0].rearrange("p n t -> p (n t)").bitcast(I32)

    def deal(dst, src, run):
        nc.vector.tensor_copy(
            dst.rearrange("p (t c i) -> p c t i", t=PACK, i=run), src.rearrange("p (c i t) -> p c t i", t=PACK, i=run)
        )

    def entries(offsets, first, count):
        return offsets[:, first // 16 : (first + count) // 16]

    def weave_out(ap):
        return ap.rearrange("p (c i t) -> p c t i", i=4, t=PACK)

    def weave_in(ap):
        return ap.rearrange("p t (c i) -> p c t i", i=4)

    with ExitStack() as ctx:
        lists = ctx.enter_context(tc.tile_pool(name="lists", bufs=1))
        keep = ctx.enter_context(tc.tile_pool(name="keep", bufs=1))
        psum = ctx.enter_context(tc.psum_pool(name="psum", bufs=1))

        def sb(name, width, dtype, tag=None):
            return keep.tile([P, width], dtype, name=name, tag=tag or name, align_bytes=64)

        offs_sb = lists.tile([P, S // 16], U16, name="offs_sb")
        kq_sb = lists.tile([P, H // 16], U16, name="kq_sb")
        rt_sb = lists.tile([P, S // 16], U16, name="rt_sb")
        lf_sb = lists.tile([P, S // 16], U16, name="lf_sb")

        x_word_table = sb("x_word_table", T, U32)
        x_byte_table = sb("x_byte_table", T, U8)
        d_byte_table = sb("d_byte_table", G, U8)
        d_word_table = sb("d_word_table", G, U32)
        w_words_raw = sb("w_words_raw", H, U32)
        w_bytes_raw = sb("w_bytes_raw", H, U8)
        d_plane = sb("d_plane", H, U8)
        gs_sb = sb("gs_sb", PACK, F32)
        gs_neg = sb("gs_neg", PACK, F32)

        nc.vector.memset(w_bytes_raw[:].bitcast(I32), 0)
        nc.gpsimd.memset(d_plane[:].bitcast(I32), 0)

        nc.sync.dma_start(kq_sb[:], kq)
        nc.sync.dma_start(d_byte_table[:].bitcast(I32), d_scales[0].bitcast(I32).unsqueeze(1).broadcast_to([16, 8, G // 4]))
        nc.sync.dma_start(offs_sb[:], offs)
        for q in range(4):
            rows = x_scales[0, 4 * q : 4 * q + 4, :].bitcast(I32)
            nc.sync.dma_start(x_byte_table[32 * q : 32 * q + 32, :].bitcast(I32), rows.unsqueeze(0).broadcast_to([8, 4, T // 4]))
        nc.sync.dma_start(x_word_table[:].bitcast(I32), as_words(x_words))
        nc.sync.dma_start(w_words_raw[:].bitcast(I32), as_words(w1_words))
        for q in range(4):
            nc.sync.dma_start(w_bytes_raw[32 * q : 32 * q + 4, :].bitcast(I32), w1_scales[0, 4 * q : 4 * q + 4, :].bitcast(I32))
        nc.sync.dma_start(d_word_table[:].bitcast(I32), as_words(d_words))
        nc.sync.dma_start(rt_sb[:], rt)
        nc.sync.dma_start(lf_sb[:], lf)
        nc.sync.dma_start(gs_sb[:], gs.rearrange("(p t) o -> p (t o)", t=PACK))

        x_codes = sb("x_codes", S, U32)
        x_plane = sb("x_plane", S, U8)
        w_codes = sb("w_codes", H, U32)
        w_plane = sb("w_plane", H, U8)
        d_picked_words = sb("d_picked_words", H, U32)
        d_picked_bytes = sb("d_picked_bytes", H, U8)
        d_codes = sb("d_codes", H, U32)
        d_dealt_bytes = sb("d_dealt_bytes", H, U8)

        nc.vector.tensor_copy(d_picked_bytes[:], d_byte_table[:].indirect(kq_sb[:]))
        nc.vector.tensor_copy(x_plane[:], x_byte_table[:].indirect(offs_sb[:]))
        nc.vector.tensor_copy(x_codes[:], x_word_table[:].indirect(offs_sb[:]))
        deal(w_codes[:].bitcast(I32), w_words_raw[:].bitcast(I32), 4)
        deal(w_plane[:], w_bytes_raw[:], 16)
        deal(d_dealt_bytes[:], d_picked_bytes[:], 16)

        y = [psum.tile([P, S], F32, name=f"y{t}", tag=f"y{t}") for t in range(PACK)]
        for t in range(PACK):
            cols = slice(P * t, P * (t + 1))
            nc.tensor.matmul_mx(
                y[t][:], lhsT=w_codes[:, cols].bitcast(FP8X4), lhsT_scale=w_plane[:, cols],
                rhs=x_codes[:].bitcast(FP8X4), rhs_scale=x_plane[:], start=True, stop=True,
            )

        nc.vector.tensor_copy(d_picked_words[:], d_word_table[:].indirect(kq_sb[:]))
        for r in range(4):
            nc.sync.dma_start(d_plane[r:P:32, :].bitcast(I32), d_dealt_bytes[8 * r : P : 32, :].bitcast(I32))

        nc.scalar.activation(gs_neg[:], gs_sb[:], ACT.Copy, scale=-1.0)

        right = [sb(f"right{t}", 2 * S, F32) for t in range(PACK)]
        there = [right[t][:, :S] for t in range(PACK)]
        sq = [right[t][:, S:] for t in range(PACK)]
        here = [sb(f"here{t}", S, F32) for t in range(PACK)]
        uh = [sb(f"uh{t}", S, F32) for t in range(PACK)]
        flux = [sb(f"flux{t}", S, F32) for t in range(PACK)]
        flux_window = [sb(f"flux_window{t}", S, F32) for t in range(PACK)]
        flux_plain = [sb(f"flux_plain{t}", S, F32) for t in range(PACK)]

        for t in range(PACK):
            nc.scalar.activation(sq[t], y[t][:], ACT.Square, scale=0.5)

        def make_there(t):
            nc.vector.scalar_tensor_tensor(there[t], y[t][:], 0.5, sq[t], ALU.mult, ALU.subtract)

        def make_here(t):
            nc.vector.scalar_tensor_tensor(here[t][:], y[t][:], 0.5, sq[t], ALU.mult, ALU.add)

        def first_half_step(t):
            nc.vector.tensor_tensor(uh[t][:], right[t][:].indirect(rt_sb[:]), here[t][:], ALU.add)
            nc.scalar.activation(flux[t][:], uh[t][:], ACT.Square, scale=0.5)
            nc.scalar.activation(flux_window[t][:], flux[t][:], ACT.Copy, scale=gs_neg[:, t : t + 1])
            for cols in [slice(0, S)] if t + 1 < PACK else [slice(0, S // 2), slice(S // 2, S)]:
                nc.scalar.activation(flux_plain[t][:, cols], flux[t][:, cols], ACT.Copy, scale=gs_neg[:, t : t + 1])

        make_there(0)
        make_here(0)
        deal(d_codes[:].bitcast(I32), d_picked_words[:].bitcast(I32), 4)
        for t in range(PACK):
            if t + 1 < PACK:
                make_there(t + 1)
            first_half_step(t)
            if t + 1 < PACK:
                make_here(t + 1)

        out_codes = sb("out_codes", S, U32)
        out_plane = sb("out_plane", S, U8)
        out_rows = out_0.rearrange("(p t) j -> p t j", t=PACK)
        out_words = as_words(out_1)

        last = PIECES - 1
        z_woven = [sb(f"z_woven{c}", PACK * PIECE, BF16) for c in range(PIECES)]
        z_codes = [sb(f"z_codes{c}", PIECE, U32) for c in range(PIECES)]
        z_plane = [sb(f"z_plane{c}", PIECE, U8) for c in range(PIECES)]
        res = [keep.tile([P, PACK, PIECE], F32, name=f"res{c}", align_bytes=64) for c in range(PIECES)]
        res_woven = [sb(f"res_woven{c}", PACK * PIECE, BF16) for c in range(PIECES)]
        z = {}
        banks = {}

        def span(c):
            return slice(PIECE * c, PIECE * (c + 1))

        z_tags = ["z0", "z1", f"flux{PACK - 1}", "z_woven0"]

        def second_half_step(c, planes):
            for t in planes:
                if t == 0:
                    z[c] = keep.tile([P, PACK, PIECE], F32, name=f"z{c}", tag=z_tags[c], align_bytes=64)
                nc.vector.tensor_tensor(
                    z[c][:, t, :], flux_window[t][:].indirect(entries(lf_sb, PIECE * c, PIECE)), flux_plain[t][:, span(c)], ALU.subtract
                )

        def second_product(c):
            nc.vector.quantize_mx(z_codes[c][:].bitcast(FP8X4), z_plane[c][:], z_woven[c][:])
            count = PACK if c == last else 1
            per_bank = PACK // count
            banks[c] = [psum.tile([P, per_bank, PIECE], F32, name=f"acc{c}_{b}", tag=f"acc{c}" if b == 0 else f"y{b}") for b in range(count)]
            for t in range(PACK):
                cols = slice(P * t, P * (t + 1))
                nc.tensor.matmul_mx(
                    banks[c][t // per_bank][:, t % per_bank, :], lhsT=d_codes[:, cols].bitcast(FP8X4), lhsT_scale=d_plane[:, cols],
                    rhs=z_codes[c][:].bitcast(FP8X4), rhs_scale=z_plane[c][:], start=True, stop=True,
                )

        def store_result(c):
            per_bank = PACK // len(banks[c])
            for b, bank in enumerate(banks[c]):
                nc.scalar.activation(res[c][:, b * per_bank : (b + 1) * per_bank, :], bank[:], ACT.Copy, scale=0.0625)
            nc.sync.dma_start(out_rows[:, :, span(c)], res[c][:])

        def weave_from_bank(c):
            nc.scalar.activation(
                res_woven[c][:].rearrange("p (n t) -> p n t", t=PACK), banks[c][0][:].rearrange("p t n -> p n t"), ACT.Copy, scale=0.0625
            )

        def quantize_result(c):
            nc.vector.quantize_mx(out_codes[:, span(c)].bitcast(FP8X4), out_plane[:, span(c)], res_woven[c][:])

        for c in (0, 1):
            second_half_step(c, range(PACK - 1))
        for c in (0, 1):
            second_half_step(c, [PACK - 1])
            nc.scalar.copy(weave_out(z_woven[c][:]), weave_in(z[c][:]))
        second_half_step(2, range(PACK))
        nc.scalar.copy(weave_out(z_woven[2][:]), weave_in(z[2][:]))
        second_product(0)
        second_product(1)
        second_half_step(last, range(PACK))
        second_product(2)
        nc.vector.tensor_copy(weave_out(z_woven[last][:]), weave_in(z[last][:]))
        second_product(last)
        for c in range(PIECES):
            store_result(c)
            if c == 0:
                weave_from_bank(c)
            else:
                nc.vector.tensor_copy(weave_out(res_woven[c][:]), weave_in(res[c][:]))
            quantize_result(c)
            if c >= last - 1:
                cols = slice(0, PIECE * last) if c < last else span(last)
                nc.sync.dma_start(out_words[:, cols], out_codes[:, cols].bitcast(I32))
        for q in range(4):
            queue = nc.scalar if q % 2 == 0 else nc.sync
            queue.dma_start(out_2[0, 4 * q : 4 * q + 4, :].bitcast(I32), out_plane[32 * q : 32 * q + 4, :].bitcast(I32))
